import numpy as np, ml_dtypes
CORES = [22,46,70,150,174,198,278,302,326,406,430,454]
N = 12
import mx_ref
NC, KT = 256, 1
OWNER = [11,11,11,1,1,1,1,1,11,1,1,1]
BF = ml_dtypes.bfloat16
def setup_inputs(rng):
    def f(*shape):
        return mx_ref.flush((rng.standard_normal(shape, dtype=np.float32) * np.exp2(rng.integers(-2, 3, shape[:-1] + (1,)))).astype(BF))
    return {"w": f(N, 128, KT * 512), "x": f(N, 128, KT * 4 * NC)}
def setup_inputs_blocks(rng):
    d = setup_inputs(rng)
    for k in ("w", "x"): d[k] = mx_ref.spread(d[k], rng, 4)
    return d
def setup_inputs_wide(rng):
    d = setup_inputs(rng)
    for k in ("w", "x"): d[k] = mx_ref.flush((d[k].astype(np.float32) * np.exp2(rng.integers(-8, 9, (N, 1, 1))).astype(np.float32)).astype(BF))
    return d
def setup_inputs_zeros(rng):
    d = setup_inputs(rng); v = d["x"].reshape(N, 128, -1, 4).copy()
    v[np.broadcast_to((rng.random((N, 1, v.shape[2], 1)) < 0.33), v.shape)] = 0
    d["x"] = v.reshape(d["x"].shape)
    return d
def reference(w, x):
    y = np.zeros((N, 128, NC), np.float32)
    for r in range(N):
        for t in range(KT):
            p = mx_ref.matmul(mx_ref.quantize(w[OWNER[r]][:, 512 * t:512 * t + 512]), mx_ref.quantize(x[r][:, 4 * NC * t:4 * NC * t + 4 * NC]))
            y[r] = p if t == 0 else y[r] + p
    return {"y": y}

from concourse.bass import DstId, RemoteDMATransfer
from concourse.mybir import dt

SCRATCH = {
    "wt": ("sbuf", [128, 512], "bfloat16"),
    "xt": ("sbuf", [128, 1024], "bfloat16"),
    "wq": ("sbuf", [128, 128], "float8_e4m3fn_x4"),
    "ws": ("sbuf", [128, 128], "uint8"),
    "rq": ("sbuf", [128, 128], "float8_e4m3fn_x4"),
    "rs": ("sbuf", [128, 128], "uint8"),
    "xq": ("sbuf", [128, 256], "float8_e4m3fn_x4"),
    "xs": ("sbuf", [128, 256], "uint8"),
    "acc": ("psum", [128, 512], "float32"),
    "yt": ("sbuf", [128, 256], "float32"),
}
SEMAPHORES = ["wl", "xl", "wqd", "xqd", "pl", "cd", "sent", "mm", "cp", "st"]

DIRECT = 5
PASS = (2, 1)


def links(topo, a, b):
    if topo.host(a) == topo.host(b) and topo.chip(a) == topo.chip(b):
        return 0
    if topo.rack(topo.host(a)) == topo.rack(topo.host(b)):
        return 1 if (topo.same_plane(a, b) or topo.mates(a, b)) else 2
    if topo.chip(a) == topo.chip(b):
        return 1
    twin = b + (topo.host(a) - topo.host(b)) * topo.CORES_PER_HOST
    return 1 + links(topo, a, twin)


def plan(T, topo):
    cores, owner = T.cores, T.tables["OWNER"]
    sends, parent = {}, {}

    def ln(a, b):
        return links(topo, cores[a], cores[b])

    def ok(a, b):
        return topo.may_write(cores[a], cores[b])

    for o in sorted(set(owner)):
        dests = [r for r in range(len(cores)) if owner[r] == o and r != o]
        near = sorted([d for d in dests if ok(o, d)], key=lambda d: (ln(o, d), d))
        fwd = [d for d in dests if d not in near]
        while len(near) > DIRECT and len(fwd) < sum(PASS):
            fwd.append(near.pop())
        groups = []
        if fwd:
            best = None
            for r1 in near:
                for r2 in near:
                    if r2 == r1:
                        continue
                    for k in range(len(fwd)):
                        a1 = [d for d in fwd if d != fwd[k]]
                        a2 = [fwd[k]]
                        if len(a1) > PASS[0] or not all(ok(r1, d) for d in a1) or not ok(r2, a2[0]):
                            continue
                        cost = sum(ln(o, r1) + ln(r1, d) for d in a1) + ln(o, r2) + ln(r2, a2[0])
                        if best is None or cost < best[0]:
                            best = (cost, r1, a1, r2, a2)
            _, r1, a1, r2, a2 = best
            groups = [[r1], [r2]]
            for r, a in ((r1, a1), (r2, a2)):
                if a:
                    sends.setdefault(r, []).append((False, a))
                    for d in a:
                        parent[d] = (r, a)
            near = [d for d in near if d not in (r1, r2)]
        if near:
            groups.append(near)
        for grp in groups:
            sends.setdefault(o, []).insert(len([s for s in sends.get(o, []) if s[0]]), (True, grp))
            for d in grp:
                parent[d] = (o, grp)
    return sends, parent


def group_mask(T, topo, sender, grp):
    m = topo.mask(T.cores[sender], T.cores[grp[0]])
    for d in grp[1:]:
        m &= topo.mask(T.cores[sender], T.cores[d])
    return m


def engines(mask):
    return bin(mask).count("1")


def rank_program(g, core, T, topo):
    rank = T.rank_of(core)
    if rank is None:
        return
    S = T.sem
    owner = T.tables["OWNER"]
    sends, parent = plan(T, topo)
    holds = rank in owner
    own = owner[rank] == rank

    if holds:
        g.sync.dma_start(T.wt[:], T.w[:]).then_inc(S.wl, 16)
    g.sync.dma_start(T.xt[:], T.x[:]).then_inc(S.xl, 16)

    if holds:
        g.vector.wait_ge(S.wl, 16)
        g.vector.quantize_mx(T.wq[:], T.ws[:], T.wt[:]).then_inc(S.wqd, 1)
    g.vector.wait_ge(S.xl, 16)
    g.vector.quantize_mx(T.xq[:], T.xs[:], T.xt[:]).then_inc(S.xqd, 1)

    landed = 0
    if not own:
        landed = engines(group_mask(T, topo, parent[rank][0], parent[rank][1]))

    def send(src, dst, sem, grp):
        mask = group_mask(T, topo, rank, grp)
        ids = [topo.addr(T.cores[d], core) for d in grp]
        if len(grp) == 1:
            g.remote_dma(dst, src, sem, S.sent, ids[0][1], ids[0][0], mask)
        else:
            g.remote_dma_fused([RemoteDMATransfer(dst_ids=[DstId(rid=r, pnc=p) for r, p in ids], dma_engine_mask=mask,
                                                  remote_sem=sem, srcs=[src], dsts=[dst] * len(grp))], local_sem=S.sent)
        return engines(mask)

    left = 0
    seen = {True: False, False: False}
    land_q, land_s = T.rq[:].bitcast(dt.uint8), T.rs[:]
    for mine, grp in sends.get(rank, []):
        if mine:
            if not seen[True]:
                g.wait_ge(S.wqd, 1)
            left += send(T.ws[:], land_s, S.pl, grp)
            left += send(T.wq[:].bitcast(dt.uint8), land_q, S.cd, grp)
        else:
            if not seen[False]:
                g.wait_ge(S.pl, landed)
            left += send(T.rs[:], land_s, S.pl, grp)
            if not seen[False]:
                g.wait_ge(S.cd, landed)
            left += send(T.rq[:].bitcast(dt.uint8), land_q, S.cd, grp)
        seen[mine] = True
    if holds and not seen[True]:
        g.wait_ge(S.wqd, 1)
    if left:
        g.wait_ge(S.sent, left)

    g.tensor.wait_ge(S.xqd, 1)
    if own:
        g.tensor.wait_ge(S.wqd, 1)
        lq, ls = T.wq[:], T.ws[:]
    else:
        g.tensor.wait_ge(S.pl, landed)
        g.tensor.wait_ge(S.cd, landed)
        lq, ls = T.rq[:], T.rs[:]
    g.tensor.matmul_mx(T.acc[:, 0:256], lq, ls, T.xq[:], T.xs[:], True, True).then_inc(S.mm, 1)

    g.vector.wait_ge(S.mm, 1)
    g.vector.tensor_copy(T.yt[:], T.acc[:, 0:256]).then_inc(S.cp, 1)
    g.sync.wait_ge(S.cp, 1)
    g.sync.dma_start(T.y[:], T.yt[:]).then_inc(S.st, 16)
    g.sync.wait_ge(S.st, 16)
